import numpy as np
import ml_dtypes


def mxq(x, axis, fmt="e4m3"):
    dtype, down = {"e4m3": (ml_dtypes.float8_e4m3fn, 7), "e5m2": (ml_dtypes.float8_e5m2, 14)}[fmt]
    v = np.moveaxis(np.asarray(x, np.float32).astype(ml_dtypes.bfloat16).astype(np.float64), axis, -1)
    blocks = v.reshape(v.shape[:-1] + (-1, 32))
    amax = np.abs(blocks).max(-1, keepdims=True)
    byte = np.maximum(np.where(amax > 0, np.frexp(amax)[1] - 1 + 127, 0) - down, 1)
    scale = np.exp2(byte - 127.0)
    codes = (blocks / scale).astype(np.float32).astype(dtype).astype(np.float64)
    return np.moveaxis((codes * scale).reshape(v.shape), -1, axis)


WIDE = False


def mx_kscale(k):
    if not WIDE:
        return np.ones(k)
    levels = np.array([10, -10, 5, -5, 0])
    if k % 512:
        return np.exp2(np.random.permutation(np.resize(levels, k // 32))).repeat(32)
    a = np.empty((k // 512, 16))
    for p in range(k // 512):
        a[p, :8] = np.random.permutation(np.resize(levels, 8))
        for g in range(8):
            far = levels[np.abs(levels - a[p, g]) >= 10]
            a[p, g + 8] = far[np.random.randint(len(far))]
    return np.exp2(a.ravel()).repeat(32)


def f64(x):
    return np.asarray(x).astype(np.float64)


def striped(idx):
    return np.tile(idx.reshape(-1, 16).T, (8, 1)).astype(np.uint16)


def unstriped(offs):
    return offs[:16].T.reshape(-1).astype(np.int64)


def striped8(idx):
    return np.concatenate([x.reshape(-1, 16).T for x in idx]).astype(np.uint16)


def runs(offs, k):
    lists = np.stack([offs[16 * r : 16 * r + 16].T.reshape(-1) for r in range(8)]).astype(np.int64)
    return lists[np.arange(k) % 512 // 64]


def pack_weight(w):
    k, n = w.shape
    w = f64(np.asarray(w, np.float32).astype(ml_dtypes.bfloat16)).reshape(k // 32, 32, n)
    amax = np.abs(w).max(1)
    byte = np.clip(np.where(amax > 0, np.frexp(amax)[1] - 1 + 127 - 7, 1), 1, 254)
    scaled = (w * np.exp2(127.0 - byte)[:, None, :]).reshape(k, n).astype(np.float32)
    words = np.ascontiguousarray(scaled.reshape(k // 512, 128, 4, n).transpose(0, 1, 3, 2)).astype(ml_dtypes.float8_e4m3fn).view(np.uint8)
    return words, np.ascontiguousarray(byte.astype(np.uint8).reshape(k // 512, 16, n))


def unpack_weight(words, scales):
    g, p, n, _ = words.shape
    vals = np.ascontiguousarray(words).view(ml_dtypes.float8_e4m3fn).astype(np.float64) * np.repeat(np.exp2(scales.astype(np.float64) - 127.0), 8, axis=1)[..., None]
    return vals.transpose(0, 1, 3, 2).reshape(g * 512, n)


K, T, S, G, H, W = 512, 1024, 256, 2048, 512, 128


def setup_inputs():
    n = np.random.standard_normal
    s = mx_kscale(K)[:, None]
    packed_xT = pack_weight(n((K, T)) * s)
    packed_dT = pack_weight(n((K, G)) / s)
    perm = np.random.permutation(S)
    perm2 = np.random.permutation(S)
    perm3 = np.random.permutation(S)
    perm4 = np.random.permutation(S)
    return {
        "x_words": packed_xT[0],
        "x_scales": packed_xT[1],
        "d_words": packed_dT[0],
        "d_scales": packed_dT[1],
        "gs": (np.random.uniform(0.5, 1.5, (K, 1)) * s).astype(np.float32),
        "offs": striped(np.random.permutation(T)[:S]),
        "k1": striped8(np.random.randint(0, G, (8, H))),
        "two": striped(np.random.permutation(T)[:S]),
        "k2": striped8(np.random.randint(0, G, (8, H))),
        "n1": striped(perm[:W]),
        "n2": striped(perm[W:]),
        "n3": striped(perm2[:W]),
        "n4": striped(perm2[W:]),
        "n5": striped(np.random.permutation(S)),
        "k3": striped8(np.random.randint(0, G, (8, H))),
        "k4": striped8(np.random.randint(0, G, (8, H))),
        "hz": striped8(np.random.randint(0, T, (8, S))),
        "n6": striped(perm3[:W]),
        "n7": striped(perm3[W:]),
        "n8": striped(perm4[:W]),
        "n9": striped(perm4[W:]),
        "n10": striped(np.random.permutation(S)),
    }


def reference(x_words, x_scales, d_words, d_scales, gs, offs, k1, two, k2, n1, n2, n3, n4, n5, k3, k4, hz, n6, n7, n8, n9, n10):
    d_k3 = unpack_weight(d_words, d_scales)[np.arange(K)[:, None], runs(k3, K)]
    d_k1 = unpack_weight(d_words, d_scales)[np.arange(K)[:, None], runs(k1, K)]
    xq = unpack_weight(x_words, x_scales)[:, unstriped(offs)]
    d_k2 = unpack_weight(d_words, d_scales)[np.arange(K)[:, None], runs(k2, K)]
    x_two = unpack_weight(x_words, x_scales)[:, unstriped(two)]
    h = 0.0625 * (d_k1.T @ xq + d_k2.T @ x_two)
    pa = h[:, unstriped(n1)]
    pb = h[:, unstriped(n2)]
    rb = np.minimum(pa, pb)
    ra = pa - pb
    ua = np.zeros((H, S))
    ua[:, unstriped(n3)] = ra
    ub = ua.copy()
    ub[:, unstriped(n4)] = rb
    z = f64(gs) * (np.maximum(ub, ub[:, unstriped(n5)]))
    d_k4 = unpack_weight(d_words, d_scales)[np.arange(K)[:, None], runs(k4, K)]
    x_hz = unpack_weight(x_words, x_scales)[np.arange(K)[:, None], runs(hz, K)]
    h2 = 0.0625 * ((d_k3.T @ mxq(z, 0, "e4m3") + d_k4.T @ x_hz))
    pa2 = h2[:, unstriped(n6)]
    pb2 = h2[:, unstriped(n7)]
    rb2 = np.maximum(pa2, pb2)
    ua2 = np.zeros((H, S))
    ua2[:, unstriped(n8)] = pb2
    ub2 = ua2.copy()
    ub2[:, unstriped(n9)] = rb2
    return ub2 - h2[:, unstriped(n10)]

@@ -1,0 +1,221 @@
+from contextlib import ExitStack
+
+import concourse.mybir as mybir
+
+K, T, S, G, H, W = 512, 1024, 256, 2048, 512, 128
+FLOPS = 4 * 2 * K * H * S
+
+F32 = mybir.dt.float32
+BF16 = mybir.dt.bfloat16
+I32 = mybir.dt.int32
+U32 = mybir.dt.uint32
+U16 = mybir.dt.uint16
+U8 = mybir.dt.uint8
+FP8X4 = mybir.dt.float8_e4m3fn_x4
+ALU = mybir.AluOpType
+COPY = mybir.ActivationFunctionType.Copy
+
+P = 128
+PACK = 4
+TILES = H // P
+PIECE = 256
+SIXTEENTH = 0.0625
+
+
+def tile_picked_mttzmhcpgfcpsw_none_p_kernel(
+    tc, x_words, x_scales, d_words, d_scales, gs, offs, k1, two, k2, n1, n2, n3, n4, n5,
+    k3, k4, hz, n6, n7, n8, n9, n10, out,
+):
+    nc = tc.nc
+    with ExitStack() as ctx:
+        lists = ctx.enter_context(tc.tile_pool(name="lists", bufs=1))
+        keep = ctx.enter_context(tc.tile_pool(name="keep", bufs=1))
+        psum = ctx.enter_context(tc.psum_pool(name="psum", bufs=1))
+
+        def load_list(src, name):
+            tile = lists.tile(list(src.shape), U16, name=name)
+            nc.sync.dma_start(tile[:], src)
+            return tile
+
+        def entries(tile, start, count):
+            return tile[:, start // 16 : (start + count) // 16]
+
+        x_bytes = keep.tile([P, T], U8, name="x_bytes")
+        d_bytes = keep.tile([P, G], U8, name="d_bytes")
+
+        def load_scales(tile, scales):
+            rows = scales[0].bitcast(I32)
+            nc.sync.dma_start(tile[:].bitcast(I32), rows.unsqueeze(1).to_broadcast([16, 8, rows.shape[1]]))
+
+        load_scales(x_bytes, x_scales)
+        l_offs, l_two = load_list(offs, "l_offs"), load_list(two, "l_two")
+        load_scales(d_bytes, d_scales)
+        l_k1, l_k2 = load_list(k1, "l_k1"), load_list(k2, "l_k2")
+
+        x_table = keep.tile([P, T], U32, name="x_table")
+        d_table = keep.tile([P, G], U32, name="d_table")
+        nc.sync.dma_start(x_table[:].bitcast(I32), x_words[0].rearrange("p n t -> p (n t)").bitcast(I32))
+        nc.sync.dma_start(d_table[:].bitcast(I32), d_words[0].rearrange("p n t -> p (n t)").bitcast(I32))
+
+        l_n1, l_n2 = load_list(n1, "l_n1"), load_list(n2, "l_n2")
+        gs_raw = keep.tile([P, PACK], F32, name="gs_raw")
+        nc.sync.dma_start(gs_raw[:], gs.rearrange("(p t) o -> p (t o)", t=PACK))
+        gain = keep.tile([P, PACK], F32, name="gain")
+        nc.vector.tensor_scalar(gain[:], gs_raw[:], SIXTEENTH, None, ALU.mult)
+        l_n3, l_n4 = load_list(n3, "l_n3"), load_list(n4, "l_n4")
+        l_k3, l_k4, l_hz = load_list(k3, "l_k3"), load_list(k4, "l_k4"), load_list(hz, "l_hz")
+        l_n5 = load_list(n5, "l_n5")
+        l_n6, l_n7 = load_list(n6, "l_n6"), load_list(n7, "l_n7")
+        l_n8, l_n9, l_n10 = load_list(n8, "l_n8"), load_list(n9, "l_n9"), load_list(n10, "l_n10")
+
+        def gather(dst, picks):
+            col = 0
+            for table, lst, count in picks:
+                for s in range(0, count, PIECE):
+                    nc.vector.tensor_copy(dst[:, col + s : col + s + PIECE], table[:].indirect(entries(lst, s, PIECE)))
+                col = col + count
+
+        def place_rows(dst, src, queues):
+            for j in range(4):
+                queues[j % len(queues)].dma_start(dst[j:P:32, :].bitcast(I32), src[8 * j : P : 32, :].bitcast(I32))
+
+        wide1 = 2 * S + 2 * H
+        bytes1 = keep.tile([P, wide1], U8, name="bytes1", tag="slot_c", align_bytes=64)
+        plane1 = keep.tile([P, wide1], U8, name="plane1", align_bytes=64)
+        nc.vector.memset(plane1[:].bitcast(I32), 0)
+        gather(bytes1, [(x_bytes, l_offs, S), (x_bytes, l_two, S), (d_bytes, l_k1, H), (d_bytes, l_k2, H)])
+        place_rows(plane1, bytes1, [nc.scalar])
+        xw1 = keep.tile([P, 2 * S], U32, name="xw1", align_bytes=64)
+        dw1 = keep.tile([P, 2 * H], U32, name="dw1")
+        gather(xw1, [(x_table, l_offs, S), (x_table, l_two, S)])
+        gather(dw1, [(d_table, l_k1, H), (d_table, l_k2, H)])
+
+        banks = []
+        words_first = keep.tile([P, 2, P], U32, name="words_first", align_bytes=64)
+        words_rest = keep.tile([P, TILES - 1, 2, P], U32, name="words_rest", tag="slot_c", align_bytes=64)
+        for t in range(TILES):
+            words_t = words_first[:] if t == 0 else words_rest[:, t - 1]
+            bytes_t = keep.tile([P, 2, P], U8, name="bytes_t%d" % t, align_bytes=64)
+            nc.vector.tensor_copy(
+                words_t.bitcast(I32),
+                dw1[:].bitcast(I32).rearrange("p (a m t) -> p a m t", a=2, t=PACK)[:, :, :, t],
+            )
+            nc.vector.tensor_copy(
+                bytes_t[:],
+                plane1[:, 2 * S :].rearrange("p (a m t) -> p a m t", a=2, t=PACK)[:, :, :, t],
+            )
+            bank = psum.tile([P, S], F32, name="h_bank%d" % t, tag="bank%d" % t)
+            for a in range(2):
+                nc.tensor.matmul_mx(
+                    out=bank[:],
+                    lhsT=words_t[:, a, :].bitcast(FP8X4),
+                    lhsT_scale=bytes_t[:, a, :],
+                    rhs=xw1[:, a * S : (a + 1) * S].bitcast(FP8X4),
+                    rhs_scale=plane1[:, a * S : (a + 1) * S],
+                    start=(a == 0),
+                    stop=(a == 1),
+                )
+            banks.append(bank)
+
+        pa = keep.tile([P, TILES, W], F32, name="pa", tag="slot_a", align_bytes=64)
+        pb = keep.tile([P, TILES, W], F32, name="pb", tag="slot_b", align_bytes=64)
+        ra = keep.tile([P, TILES, W], F32, name="ra")
+        rb = keep.tile([P, TILES, W], F32, name="rb")
+        for t in range(TILES):
+            h_t = keep.tile([P, S], F32, name="h%d" % t)
+            nc.vector.tensor_copy(h_t[:], banks[t][:])
+            nc.scalar.activation(pa[:, t, :], h_t[:].indirect(l_n1[:]), COPY)
+            nc.scalar.activation(pb[:, t, :], h_t[:].indirect(l_n2[:]), COPY)
+        for t in range(TILES):
+            nc.vector.tensor_tensor(ra[:, t, :], pa[:, t, :], pb[:, t, :], ALU.subtract)
+            nc.vector.tensor_tensor(rb[:, t, :], pa[:, t, :], pb[:, t, :], ALU.min)
+        ubs = [keep.tile([P, S], F32, name="ub%d" % t) for t in range(TILES)]
+        for t in range(TILES):
+            nc.scalar.activation(ubs[t][:].indirect(l_n3[:]), ra[:, t, :], COPY)
+        for t in range(TILES):
+            nc.scalar.activation(ubs[t][:].indirect(l_n4[:]), rb[:, t, :], COPY)
+
+        wide2 = S + 2 * H
+        bytes2 = keep.tile([P, wide2], U8, name="bytes2", tag="slot_a", align_bytes=64)
+        plane2 = keep.tile([P, wide2], U8, name="plane2", align_bytes=64)
+        nc.vector.memset(plane2[:].bitcast(I32), 0)
+        gather(bytes2, [(x_bytes, l_hz, S), (d_bytes, l_k4, H), (d_bytes, l_k3, H)])
+        place_rows(plane2, bytes2, [nc.sync])
+        words2 = keep.tile([P, wide2], U32, name="words2", tag="slot_b", align_bytes=64)
+        gather(words2, [(x_table, l_hz, S), (d_table, l_k4, H), (d_table, l_k3, H)])
+
+        banks2 = [
+            [psum.tile([P, W], F32, name="h2_bank%d_%d" % (half, t), tag="bank%d" % (half * TILES + t)) for t in range(TILES)]
+            for half in range(2)
+        ]
+        for half in range(2):
+            cols = slice(half * W, (half + 1) * W)
+            for t in range(TILES):
+                wcols = slice(S + t * P, S + (t + 1) * P)
+                nc.tensor.matmul_mx(
+                    out=banks2[half][t][:],
+                    lhsT=words2[:, wcols].bitcast(FP8X4),
+                    lhsT_scale=plane2[:, wcols],
+                    rhs=words2[:, cols].bitcast(FP8X4),
+                    rhs_scale=plane2[:, cols],
+                    start=True,
+                    stop=False,
+                )
+        h2s = [keep.tile([P, S], F32, name="h2_%d" % t) for t in range(TILES)]
+
+        for half in range(2):
+            cols = slice(half * W, (half + 1) * W)
+            far = keep.tile([P, TILES, W], F32, name="far%d" % half)
+            top = keep.tile([P, TILES, W], F32, name="top%d" % half)
+            for t in range(TILES):
+                nc.scalar.activation(far[:, t, :], ubs[t][:].indirect(entries(l_n5, half * W, W)), COPY)
+                nc.vector.tensor_tensor(top[:, t, :], ubs[t][:, cols], far[:, t, :], ALU.max)
+            z_bf = keep.tile([P, W, PACK], BF16, name="z_bf%d" % half, align_bytes=64)
+            nc.vector.tensor_tensor(
+                z_bf[:],
+                top[:].rearrange("p t c -> p c t"),
+                gain[:].unsqueeze(1).to_broadcast([P, W, PACK]),
+                ALU.mult,
+            )
+            z_words = keep.tile([P, W], U32, name="z_words%d" % half, align_bytes=64)
+            z_plane = keep.tile([P, W], U8, name="z_plane%d" % half, align_bytes=64)
+            nc.vector.quantize_mx(
+                out=z_words[:].bitcast(FP8X4),
+                scales=z_plane[:],
+                in_=z_bf[:].rearrange("p c t -> p (c t)"),
+            )
+            for t in range(TILES):
+                wcols = slice(S + H + t * P, S + H + (t + 1) * P)
+                nc.tensor.matmul_mx(
+                    out=banks2[half][t][:],
+                    lhsT=words2[:, wcols].bitcast(FP8X4),
+                    lhsT_scale=plane2[:, wcols],
+                    rhs=z_words[:].bitcast(FP8X4),
+                    rhs_scale=z_plane[:],
+                    start=False,
+                    stop=True,
+                )
+            for t in range(TILES):
+                nc.vector.tensor_scalar(h2s[t][:, cols], banks2[half][t][:], SIXTEENTH, None, ALU.mult)
+
+        pa2 = keep.tile([P, TILES, W], F32, name="pa2")
+        pb2 = keep.tile([P, TILES, W], F32, name="pb2")
+        rb2 = keep.tile([P, TILES, W], F32, name="rb2")
+        for t in range(TILES):
+            h2_t = h2s[t]
+            nc.scalar.activation(pa2[:, t, :], h2_t[:].indirect(l_n6[:]), COPY)
+            nc.scalar.activation(pb2[:, t, :], h2_t[:].indirect(l_n7[:]), COPY)
+        for t in range(TILES):
+            nc.vector.tensor_tensor(rb2[:, t, :], pa2[:, t, :], pb2[:, t, :], ALU.max)
+        for t in range(TILES):
+            ub2 = keep.tile([P, S], F32, name="ub2_%d" % t)
+            far2 = keep.tile([P, S], F32, name="far2_%d" % t)
+            res = keep.tile([P, S], F32, name="res%d" % t)
+            nc.scalar.activation(ub2[:].indirect(l_n8[:]), pb2[:, t, :], COPY)
+            nc.scalar.activation(far2[:, 0:W], h2s[t][:].indirect(entries(l_n10, 0, W)), COPY)
+            nc.scalar.activation(ub2[:].indirect(l_n9[:]), rb2[:, t, :], COPY)
+            nc.scalar.activation(far2[:, W:S], h2s[t][:].indirect(entries(l_n10, W, W)), COPY)
+            for half in range(2):
+                cols = slice(half * W, (half + 1) * W)
+                nc.vector.tensor_tensor(res[:, cols], ub2[:, cols], far2[:, cols], ALU.subtract)
+                nc.sync.dma_start(out[t * P : (t + 1) * P, cols], res[:, cols])

@@ -18,8 +18,8 @@ COPY = mybir.ActivationFunctionType.Copy
 P = 128
 PACK = 4
 TILES = H // P
-PIECE = 256
 SIXTEENTH = 0.0625
+WINDOW = S + 8
 
 
 def tile_picked_mttzmhcpgfcpsw_none_p_kernel(
@@ -30,6 +30,8 @@ def tile_picked_mttzmhcpgfcpsw_none_p_kernel(
     with ExitStack() as ctx:
         lists = ctx.enter_context(tc.tile_pool(name="lists", bufs=1))
         keep = ctx.enter_context(tc.tile_pool(name="keep", bufs=1))
+        shared = ctx.enter_context(tc.tile_pool(name="shared", bufs=1))
+        later = ctx.enter_context(tc.tile_pool(name="later", bufs=1))
         psum = ctx.enter_context(tc.psum_pool(name="psum", bufs=1))
 
         def load_list(src, name):
@@ -54,8 +56,8 @@ def tile_picked_mttzmhcpgfcpsw_none_p_kernel(
 
         x_table = keep.tile([P, T], U32, name="x_table")
         d_table = keep.tile([P, G], U32, name="d_table")
-        nc.sync.dma_start(x_table[:].bitcast(I32), x_words[0].rearrange("p n t -> p (n t)").bitcast(I32))
         nc.sync.dma_start(d_table[:].bitcast(I32), d_words[0].rearrange("p n t -> p (n t)").bitcast(I32))
+        nc.sync.dma_start(x_table[:].bitcast(I32), x_words[0].rearrange("p n t -> p (n t)").bitcast(I32))
 
         l_n1, l_n2 = load_list(n1, "l_n1"), load_list(n2, "l_n2")
         gs_raw = keep.tile([P, PACK], F32, name="gs_raw")
@@ -70,9 +72,9 @@ def tile_picked_mttzmhcpgfcpsw_none_p_kernel(
 
         def gather(dst, picks):
             col = 0
-            for table, lst, count in picks:
-                for s in range(0, count, PIECE):
-                    nc.vector.tensor_copy(dst[:, col + s : col + s + PIECE], table[:].indirect(entries(lst, s, PIECE)))
+            for table, offsets in picks:
+                count = 16 * offsets.shape[1]
+                nc.vector.tensor_copy(dst[:, col : col + count], table[:].indirect(offsets))
                 col = col + count
 
         def place_rows(dst, src, queues):
@@ -80,142 +82,204 @@ def tile_picked_mttzmhcpgfcpsw_none_p_kernel(
                 queues[j % len(queues)].dma_start(dst[j:P:32, :].bitcast(I32), src[8 * j : P : 32, :].bitcast(I32))
 
         wide1 = 2 * S + 2 * H
-        bytes1 = keep.tile([P, wide1], U8, name="bytes1", tag="slot_c", align_bytes=64)
+        bytes1 = shared.tile([P, wide1], U8, name="bytes1", align_bytes=64, offset=0)
         plane1 = keep.tile([P, wide1], U8, name="plane1", align_bytes=64)
         nc.vector.memset(plane1[:].bitcast(I32), 0)
-        gather(bytes1, [(x_bytes, l_offs, S), (x_bytes, l_two, S), (d_bytes, l_k1, H), (d_bytes, l_k2, H)])
+        gather(bytes1, [(x_bytes, l_offs[:]), (x_bytes, l_two[:]), (d_bytes, l_k1[:]), (d_bytes, l_k2[:])])
         place_rows(plane1, bytes1, [nc.scalar])
-        xw1 = keep.tile([P, 2 * S], U32, name="xw1", align_bytes=64)
         dw1 = keep.tile([P, 2 * H], U32, name="dw1")
-        gather(xw1, [(x_table, l_offs, S), (x_table, l_two, S)])
-        gather(dw1, [(d_table, l_k1, H), (d_table, l_k2, H)])
+        gather(dw1, [(d_table, l_k1[:]), (d_table, l_k2[:])])
+        dealt_words = [
+            keep.tile([P, 2, 2, P], U32, name="dealt_words0", align_bytes=64),
+            shared.tile([P, 2, 2, P], U32, name="dealt_words1", align_bytes=64, offset=4 * S),
+        ]
+        dealt_bytes = [keep.tile([P, 2, 2, P], U8, name="dealt_bytes%d" % i, align_bytes=64) for i in range(2)]
 
-        banks = []
-        words_first = keep.tile([P, 2, P], U32, name="words_first", align_bytes=64)
-        words_rest = keep.tile([P, TILES - 1, 2, P], U32, name="words_rest", tag="slot_c", align_bytes=64)
-        for t in range(TILES):
-            words_t = words_first[:] if t == 0 else words_rest[:, t - 1]
-            bytes_t = keep.tile([P, 2, P], U8, name="bytes_t%d" % t, align_bytes=64)
+        def deal(i):
+            tiles = slice(2 * i, 2 * i + 2)
             nc.vector.tensor_copy(
-                words_t.bitcast(I32),
-                dw1[:].bitcast(I32).rearrange("p (a m t) -> p a m t", a=2, t=PACK)[:, :, :, t],
+                dealt_words[i][:].bitcast(I32).rearrange("p a t m -> p a m t"),
+                dw1[:].bitcast(I32).rearrange("p (a m t) -> p a m t", a=2, t=PACK)[:, :, :, tiles],
             )
             nc.vector.tensor_copy(
-                bytes_t[:],
-                plane1[:, 2 * S :].rearrange("p (a m t) -> p a m t", a=2, t=PACK)[:, :, :, t],
+                dealt_bytes[i][:].rearrange("p a t m -> p a m t"),
+                plane1[:, 2 * S :].rearrange("p (a m t) -> p a m t", a=2, t=PACK)[:, :, :, tiles],
             )
-            bank = psum.tile([P, S], F32, name="h_bank%d" % t, tag="bank%d" % t)
+
+        xw_offs = keep.tile([P, S], U32, name="xw_offs", align_bytes=64)
+        xw_two = shared.tile([P, S], U32, name="xw_two", align_bytes=64, offset=0)
+        xw1 = [xw_offs, xw_two]
+        deal(0)
+        gather(xw_offs, [(x_table, l_offs[:])])
+        gather(xw_two, [(x_table, l_two[:])])
+        deal(1)
+        banks = [psum.tile([P, S], F32, name="h_bank%d" % t, tag="bank%d" % t) for t in range(TILES)]
+        for i in range(2):
             for a in range(2):
-                nc.tensor.matmul_mx(
-                    out=bank[:],
-                    lhsT=words_t[:, a, :].bitcast(FP8X4),
-                    lhsT_scale=bytes_t[:, a, :],
-                    rhs=xw1[:, a * S : (a + 1) * S].bitcast(FP8X4),
-                    rhs_scale=plane1[:, a * S : (a + 1) * S],
-                    start=(a == 0),
-                    stop=(a == 1),
-                )
-            banks.append(bank)
+                for t in range(2):
+                    nc.tensor.matmul_mx(
+                        out=banks[2 * i + t][:],
+                        lhsT=dealt_words[i][:, a, t, :].bitcast(FP8X4),
+                        lhsT_scale=dealt_bytes[i][:, a, t, :],
+                        rhs=xw1[a][:].bitcast(FP8X4),
+                        rhs_scale=plane1[:, a * S : (a + 1) * S],
+                        start=(a == 0),
+                        stop=(a == 1),
+                    )
 
-        pa = keep.tile([P, TILES, W], F32, name="pa", tag="slot_a", align_bytes=64)
-        pb = keep.tile([P, TILES, W], F32, name="pb", tag="slot_b", align_bytes=64)
+        pab = [
+            later.tile([P, 2, 2, W], F32, name="pab0", align_bytes=64, offset=256),
+            keep.tile([P, 2, 2, W], F32, name="pab1"),
+        ]
         ra = keep.tile([P, TILES, W], F32, name="ra")
         rb = keep.tile([P, TILES, W], F32, name="rb")
         for t in range(TILES):
             h_t = keep.tile([P, S], F32, name="h%d" % t)
-            nc.vector.tensor_copy(h_t[:], banks[t][:])
-            nc.scalar.activation(pa[:, t, :], h_t[:].indirect(l_n1[:]), COPY)
-            nc.scalar.activation(pb[:, t, :], h_t[:].indirect(l_n2[:]), COPY)
-        for t in range(TILES):
-            nc.vector.tensor_tensor(ra[:, t, :], pa[:, t, :], pb[:, t, :], ALU.subtract)
-            nc.vector.tensor_tensor(rb[:, t, :], pa[:, t, :], pb[:, t, :], ALU.min)
-        ubs = [keep.tile([P, S], F32, name="ub%d" % t) for t in range(TILES)]
-        for t in range(TILES):
+            if t == 0:
+                nc.scalar.activation(h_t[:], banks[t][:], COPY)
+            else:
+                nc.vector.tensor_copy(h_t[:], banks[t][:])
+            nc.scalar.activation(pab[t // 2][:, 0, t % 2, :], h_t[:].indirect(l_n1[:]), COPY)
+            nc.scalar.activation(pab[t // 2][:, 1, t % 2, :], h_t[:].indirect(l_n2[:]), COPY)
+
+        def combine(i):
+            two_tiles = slice(2 * i, 2 * i + 2)
+            nc.vector.tensor_tensor(ra[:, two_tiles, :], pab[i][:, 0], pab[i][:, 1], ALU.subtract)
+            nc.vector.tensor_tensor(rb[:, two_tiles, :], pab[i][:, 0], pab[i][:, 1], ALU.min)
+
+        combine(0)
+        ubs = [keep.tile([P, WINDOW], F32, name="ub%d" % t) for t in range(TILES)]
+        last = TILES - 1
+        far = keep.tile([P, 2, 2, W], F32, name="far")
+        top = keep.tile([P, 2, TILES, W], F32, name="top")
+
+        def put_ra(t):
             nc.scalar.activation(ubs[t][:].indirect(l_n3[:]), ra[:, t, :], COPY)
-        for t in range(TILES):
+
+        def put_rb(t):
             nc.scalar.activation(ubs[t][:].indirect(l_n4[:]), rb[:, t, :], COPY)
 
+
         wide2 = S + 2 * H
-        bytes2 = keep.tile([P, wide2], U8, name="bytes2", tag="slot_a", align_bytes=64)
+        bytes2 = later.tile([P, wide2], U8, name="bytes2", align_bytes=64, offset=0)
         plane2 = keep.tile([P, wide2], U8, name="plane2", align_bytes=64)
         nc.vector.memset(plane2[:].bitcast(I32), 0)
-        gather(bytes2, [(x_bytes, l_hz, S), (d_bytes, l_k4, H), (d_bytes, l_k3, H)])
+        gather(bytes2, [(x_bytes, l_hz[:]), (d_bytes, l_k4[:]), (d_bytes, l_k3[:])])
         place_rows(plane2, bytes2, [nc.sync])
-        words2 = keep.tile([P, wide2], U32, name="words2", tag="slot_b", align_bytes=64)
-        gather(words2, [(x_table, l_hz, S), (d_table, l_k4, H), (d_table, l_k3, H)])
+        combine(1)
+        words2 = later.tile([P, wide2], U32, name="words2", align_bytes=64, offset=wide2)
+        gather(words2, [(x_table, l_hz[:]), (d_table, l_k4[:]), (d_table, l_k3[:])])
 
+        halves = [slice(0, W), slice(W, S)]
+        groups2 = [(0, halves[0]), (0, halves[1])] + [(t, slice(0, S)) for t in range(1, TILES)]
         banks2 = [
-            [psum.tile([P, W], F32, name="h2_bank%d_%d" % (half, t), tag="bank%d" % (half * TILES + t)) for t in range(TILES)]
-            for half in range(2)
+            psum.tile([P, cols.stop - cols.start], F32, name="h2_bank%d" % g, tag="bank%d" % ((TILES + g) % 8))
+            for g, (t, cols) in enumerate(groups2)
         ]
-        for half in range(2):
-            cols = slice(half * W, (half + 1) * W)
-            for t in range(TILES):
-                wcols = slice(S + t * P, S + (t + 1) * P)
-                nc.tensor.matmul_mx(
-                    out=banks2[half][t][:],
-                    lhsT=words2[:, wcols].bitcast(FP8X4),
-                    lhsT_scale=plane2[:, wcols],
-                    rhs=words2[:, cols].bitcast(FP8X4),
-                    rhs_scale=plane2[:, cols],
-                    start=True,
-                    stop=False,
-                )
-        h2s = [keep.tile([P, S], F32, name="h2_%d" % t) for t in range(TILES)]
+        for g, (t, cols) in enumerate(groups2):
+            wcols = slice(S + t * P, S + (t + 1) * P)
+            nc.tensor.matmul_mx(
+                out=banks2[g][:],
+                lhsT=words2[:, wcols].bitcast(FP8X4),
+                lhsT_scale=plane2[:, wcols],
+                rhs=words2[:, cols].bitcast(FP8X4),
+                rhs_scale=plane2[:, cols],
+                start=True,
+                stop=False,
+            )
+        z_words = keep.tile([P, S], U32, name="z_words", align_bytes=64)
+        z_plane = keep.tile([P, S], U8, name="z_plane", align_bytes=64)
+        h2s = [keep.tile([P, WINDOW], F32, name="h2_%d" % t) for t in range(TILES)]
 
-        for half in range(2):
-            cols = slice(half * W, (half + 1) * W)
-            far = keep.tile([P, TILES, W], F32, name="far%d" % half)
-            top = keep.tile([P, TILES, W], F32, name="top%d" % half)
-            for t in range(TILES):
-                nc.scalar.activation(far[:, t, :], ubs[t][:].indirect(entries(l_n5, half * W, W)), COPY)
-                nc.vector.tensor_tensor(top[:, t, :], ubs[t][:, cols], far[:, t, :], ALU.max)
-            z_bf = keep.tile([P, W, PACK], BF16, name="z_bf%d" % half, align_bytes=64)
+        z_bf = [keep.tile([P, W, PACK], BF16, name="z_bf%d" % half, tag="z_bf%d" % half, align_bytes=64) for half in range(2)]
+
+        def larger_half(t, half):
+            nc.scalar.activation(far[:, half, t - 2, :], ubs[t][:].indirect(entries(l_n5, half * W, W)), COPY)
+            nc.vector.tensor_tensor(top[:, half, t, :], ubs[t][:, half * W : (half + 1) * W], far[:, half, t - 2, :], ALU.max)
+
+        def weigh(i, half):
+            tiles = slice(2 * i, 2 * i + 2)
             nc.vector.tensor_tensor(
-                z_bf[:],
-                top[:].rearrange("p t c -> p c t"),
-                gain[:].unsqueeze(1).to_broadcast([P, W, PACK]),
+                z_bf[half][:, :, tiles],
+                top[:, half, tiles, :].rearrange("p t c -> p c t"),
+                gain[:, tiles].unsqueeze(1).to_broadcast([P, W, 2]),
                 ALU.mult,
             )
-            z_words = keep.tile([P, W], U32, name="z_words%d" % half, align_bytes=64)
-            z_plane = keep.tile([P, W], U8, name="z_plane%d" % half, align_bytes=64)
-            nc.vector.quantize_mx(
-                out=z_words[:].bitcast(FP8X4),
-                scales=z_plane[:],
-                in_=z_bf[:].rearrange("p c t -> p (c t)"),
+
+        def larger_whole(t):
+            far_t = keep.tile([P, S], F32, name="far_t%d" % t)
+            nc.scalar.activation(far_t[:], ubs[t][:].indirect(l_n5[:]), COPY)
+            nc.vector.tensor_tensor(
+                top[:, :, t, :],
+                ubs[t][:, 0:S].rearrange("p (a c) -> p a c", a=2),
+                far_t[:].rearrange("p (a c) -> p a c", a=2),
+                ALU.max,
             )
-            for t in range(TILES):
-                wcols = slice(S + H + t * P, S + H + (t + 1) * P)
-                nc.tensor.matmul_mx(
-                    out=banks2[half][t][:],
-                    lhsT=words2[:, wcols].bitcast(FP8X4),
-                    lhsT_scale=plane2[:, wcols],
-                    rhs=z_words[:].bitcast(FP8X4),
-                    rhs_scale=z_plane[:],
-                    start=False,
-                    stop=True,
-                )
-            for t in range(TILES):
-                nc.vector.tensor_scalar(h2s[t][:, cols], banks2[half][t][:], SIXTEENTH, None, ALU.mult)
+
+        put_ra(0)
+        put_ra(1)
+        put_rb(0)
+        put_rb(1)
+        larger_whole(0)
+        put_ra(2)
+        larger_whole(1)
+        for half in range(2):
+            weigh(0, half)
+        put_ra(3)
+        put_rb(2)
+        put_rb(3)
+        for half in range(2):
+            larger_half(2, half)
+            larger_half(3, half)
+            weigh(1, half)
+            nc.vector.quantize_mx(
+                out=z_words[:, halves[half]].bitcast(FP8X4),
+                scales=z_plane[:, halves[half]],
+                in_=z_bf[half][:].rearrange("p c t -> p (c t)"),
+            )
+        for g, (t, cols) in enumerate(groups2):
+            wcols = slice(S + H + t * P, S + H + (t + 1) * P)
+            nc.tensor.matmul_mx(
+                out=banks2[g][:],
+                lhsT=words2[:, wcols].bitcast(FP8X4),
+                lhsT_scale=plane2[:, wcols],
+                rhs=z_words[:, cols].bitcast(FP8X4),
+                rhs_scale=z_plane[:, cols],
+                start=False,
+                stop=True,
+            )
+            if t == 0:
+                nc.scalar.activation(h2s[t][:, cols], banks2[g][:], COPY, scale=SIXTEENTH)
+            else:
+                nc.vector.tensor_scalar(h2s[t][:, cols], banks2[g][:], SIXTEENTH, None, ALU.mult)
 
         pa2 = keep.tile([P, TILES, W], F32, name="pa2")
         pb2 = keep.tile([P, TILES, W], F32, name="pb2")
         rb2 = keep.tile([P, TILES, W], F32, name="rb2")
-        for t in range(TILES):
-            h2_t = h2s[t]
-            nc.scalar.activation(pa2[:, t, :], h2_t[:].indirect(l_n6[:]), COPY)
-            nc.scalar.activation(pb2[:, t, :], h2_t[:].indirect(l_n7[:]), COPY)
-        for t in range(TILES):
+        ub2s = [keep.tile([P, S], F32, name="ub2_%d" % t) for t in range(TILES)]
+
+        def pair_up(t):
+            nc.scalar.activation(pa2[:, t, :], h2s[t][:].indirect(l_n6[:]), COPY)
+            nc.scalar.activation(pb2[:, t, :], h2s[t][:].indirect(l_n7[:]), COPY)
             nc.vector.tensor_tensor(rb2[:, t, :], pa2[:, t, :], pb2[:, t, :], ALU.max)
-        for t in range(TILES):
-            ub2 = keep.tile([P, S], F32, name="ub2_%d" % t)
+
+        def finish(t):
+            ub2 = ub2s[t]
             far2 = keep.tile([P, S], F32, name="far2_%d" % t)
             res = keep.tile([P, S], F32, name="res%d" % t)
+            pieces = [slice(0, S)] if t < last else [slice(0, W), slice(W, S)]
             nc.scalar.activation(ub2[:].indirect(l_n8[:]), pb2[:, t, :], COPY)
-            nc.scalar.activation(far2[:, 0:W], h2s[t][:].indirect(entries(l_n10, 0, W)), COPY)
+            first = pieces[0]
+            nc.scalar.activation(far2[:, first], h2s[t][:].indirect(entries(l_n10, first.start, first.stop - first.start)), COPY)
             nc.scalar.activation(ub2[:].indirect(l_n9[:]), rb2[:, t, :], COPY)
-            nc.scalar.activation(far2[:, W:S], h2s[t][:].indirect(entries(l_n10, W, W)), COPY)
-            for half in range(2):
-                cols = slice(half * W, (half + 1) * W)
+            for cols in pieces[1:]:
+                nc.scalar.activation(far2[:, cols], h2s[t][:].indirect(entries(l_n10, cols.start, cols.stop - cols.start)), COPY)
+            for cols in pieces:
                 nc.vector.tensor_tensor(res[:, cols], ub2[:, cols], far2[:, cols], ALU.subtract)
                 nc.sync.dma_start(out[t * P : (t + 1) * P, cols], res[:, cols])
+
+        pair_up(0)
+        for t in range(TILES):
+            if t < last:
+                pair_up(t + 1)
+            finish(t)

@@ -47,7 +47,7 @@ def tile_picked_mttzmhcpgfcpsw_none_p_kernel(
 
         def load_scales(tile, scales):
             rows = scales[0].bitcast(I32)
-            nc.sync.dma_start(tile[:].bitcast(I32), rows.unsqueeze(1).to_broadcast([16, 8, rows.shape[1]]))
+            nc.scalar.dma_start(tile[:].bitcast(I32), rows.unsqueeze(1).to_broadcast([16, 8, rows.shape[1]]))
 
         load_scales(x_bytes, x_scales)
         l_offs, l_two = load_list(offs, "l_offs"), load_list(two, "l_two")
@@ -114,18 +114,17 @@ def tile_picked_mttzmhcpgfcpsw_none_p_kernel(
         gather(xw_two, [(x_table, l_two[:])])
         deal(1)
         banks = [psum.tile([P, S], F32, name="h_bank%d" % t, tag="bank%d" % t) for t in range(TILES)]
-        for i in range(2):
-            for a in range(2):
-                for t in range(2):
-                    nc.tensor.matmul_mx(
-                        out=banks[2 * i + t][:],
-                        lhsT=dealt_words[i][:, a, t, :].bitcast(FP8X4),
-                        lhsT_scale=dealt_bytes[i][:, a, t, :],
-                        rhs=xw1[a][:].bitcast(FP8X4),
-                        rhs_scale=plane1[:, a * S : (a + 1) * S],
-                        start=(a == 0),
-                        stop=(a == 1),
-                    )
+        passes = [(0, a, t) for a in range(2) for t in range(2)] + [(1, a, t) for t in range(2) for a in range(2)]
+        for i, a, t in passes:
+            nc.tensor.matmul_mx(
+                out=banks[2 * i + t][:],
+                lhsT=dealt_words[i][:, a, t, :].bitcast(FP8X4),
+                lhsT_scale=dealt_bytes[i][:, a, t, :],
+                rhs=xw1[a][:].bitcast(FP8X4),
+                rhs_scale=plane1[:, a * S : (a + 1) * S],
+                start=(a == 0),
+                stop=(a == 1),
+            )
 
         pab = [
             later.tile([P, 2, 2, W], F32, name="pab0", align_bytes=64, offset=256),
@@ -167,8 +166,9 @@ def tile_picked_mttzmhcpgfcpsw_none_p_kernel(
         gather(bytes2, [(x_bytes, l_hz[:]), (d_bytes, l_k4[:]), (d_bytes, l_k3[:])])
         place_rows(plane2, bytes2, [nc.sync])
         combine(1)
-        words2 = later.tile([P, wide2], U32, name="words2", align_bytes=64, offset=wide2)
-        gather(words2, [(x_table, l_hz[:]), (d_table, l_k4[:]), (d_table, l_k3[:])])
+        part = H // 2
+        words2 = later.tile([P, S + 2 * part], U32, name="words2", align_bytes=64, offset=wide2)
+        gather(words2, [(x_table, l_hz[:]), (d_table, entries(l_k4, 0, part)), (d_table, entries(l_k3, 0, part))])
 
         halves = [slice(0, W), slice(W, S)]
         groups2 = [(0, halves[0]), (0, halves[1])] + [(t, slice(0, S)) for t in range(1, TILES)]
@@ -176,17 +176,40 @@ def tile_picked_mttzmhcpgfcpsw_none_p_kernel(
             psum.tile([P, cols.stop - cols.start], F32, name="h2_bank%d" % g, tag="bank%d" % ((TILES + g) % 8))
             for g, (t, cols) in enumerate(groups2)
         ]
-        for g, (t, cols) in enumerate(groups2):
-            wcols = slice(S + t * P, S + (t + 1) * P)
+
+        def hashed_pass(g, words):
+            t, cols = groups2[g]
             nc.tensor.matmul_mx(
                 out=banks2[g][:],
-                lhsT=words2[:, wcols].bitcast(FP8X4),
-                lhsT_scale=plane2[:, wcols],
+                lhsT=words.bitcast(FP8X4),
+                lhsT_scale=plane2[:, S + t * P : S + (t + 1) * P],
                 rhs=words2[:, cols].bitcast(FP8X4),
                 rhs_scale=plane2[:, cols],
                 start=True,
                 stop=False,
             )
+
+        def z_pass(g, words):
+            t, cols = groups2[g]
+            nc.tensor.matmul_mx(
+                out=banks2[g][:],
+                lhsT=words.bitcast(FP8X4),
+                lhsT_scale=plane2[:, S + H + t * P : S + H + (t + 1) * P],
+                rhs=z_words[:, cols].bitcast(FP8X4),
+                rhs_scale=z_plane[:, cols],
+                start=False,
+                stop=True,
+            )
+            if t == 0:
+                nc.scalar.activation(h2s[t][:, cols], banks2[g][:], COPY, scale=SIXTEENTH)
+            else:
+                nc.vector.tensor_scalar(h2s[t][:, cols], banks2[g][:], SIXTEENTH, None, ALU.mult)
+
+        early = [g for g, (t, cols) in enumerate(groups2) if t < 2]
+        late = [g for g, (t, cols) in enumerate(groups2) if t >= 2]
+        for g in early:
+            t = groups2[g][0]
+            hashed_pass(g, words2[:, S + t * P : S + (t + 1) * P])
         z_words = keep.tile([P, S], U32, name="z_words", align_bytes=64)
         z_plane = keep.tile([P, S], U8, name="z_plane", align_bytes=64)
         h2s = [keep.tile([P, WINDOW], F32, name="h2_%d" % t) for t in range(TILES)]
@@ -237,21 +260,15 @@ def tile_picked_mttzmhcpgfcpsw_none_p_kernel(
                 scales=z_plane[:, halves[half]],
                 in_=z_bf[half][:].rearrange("p c t -> p (c t)"),
             )
-        for g, (t, cols) in enumerate(groups2):
-            wcols = slice(S + H + t * P, S + H + (t + 1) * P)
-            nc.tensor.matmul_mx(
-                out=banks2[g][:],
-                lhsT=words2[:, wcols].bitcast(FP8X4),
-                lhsT_scale=plane2[:, wcols],
-                rhs=z_words[:, cols].bitcast(FP8X4),
-                rhs_scale=z_plane[:, cols],
-                start=False,
-                stop=True,
-            )
-            if t == 0:
-                nc.scalar.activation(h2s[t][:, cols], banks2[g][:], COPY, scale=SIXTEENTH)
-            else:
-                nc.vector.tensor_scalar(h2s[t][:, cols], banks2[g][:], SIXTEENTH, None, ALU.mult)
+        for g in early:
+            t = groups2[g][0]
+            z_pass(g, words2[:, S + part + t * P : S + part + (t + 1) * P])
+        words_late = keep.tile([P, 2 * part], U32, name="words_late", tag="z_bf1", align_bytes=64)
+        gather(words_late, [(d_table, entries(l_k4, part, part)), (d_table, entries(l_k3, part, part))])
+        for g in late:
+            t = groups2[g][0] - 2
+            hashed_pass(g, words_late[:, t * P : (t + 1) * P])
+            z_pass(g, words_late[:, part + t * P : part + (t + 1) * P])
 
         pa2 = keep.tile([P, TILES, W], F32, name="pa2")
         pb2 = keep.tile([P, TILES, W], F32, name="pb2")

from contextlib import ExitStack

import concourse.mybir as mybir

K, T, S, G, H, W = 512, 1024, 256, 2048, 512, 128
FLOPS = 4 * 2 * K * H * S

F32 = mybir.dt.float32
BF16 = mybir.dt.bfloat16
I32 = mybir.dt.int32
U32 = mybir.dt.uint32
U16 = mybir.dt.uint16
U8 = mybir.dt.uint8
FP8X4 = mybir.dt.float8_e4m3fn_x4
ALU = mybir.AluOpType
COPY = mybir.ActivationFunctionType.Copy

P = 128
PACK = 4
TILES = H // P
SIXTEENTH = 0.0625
WINDOW = S + 8


def tile_picked_mttzmhcpgfcpsw_none_p_kernel(
    tc, x_words, x_scales, d_words, d_scales, gs, offs, k1, two, k2, n1, n2, n3, n4, n5,
    k3, k4, hz, n6, n7, n8, n9, n10, out,
):
    nc = tc.nc
    with ExitStack() as ctx:
        lists = ctx.enter_context(tc.tile_pool(name="lists", bufs=1))
        keep = ctx.enter_context(tc.tile_pool(name="keep", bufs=1))
        shared = ctx.enter_context(tc.tile_pool(name="shared", bufs=1))
        later = ctx.enter_context(tc.tile_pool(name="later", bufs=1))
        psum = ctx.enter_context(tc.psum_pool(name="psum", bufs=1))

        def load_list(src, name):
            tile = lists.tile(list(src.shape), U16, name=name)
            nc.sync.dma_start(tile[:], src)
            return tile

        def entries(tile, start, count):
            return tile[:, start // 16 : (start + count) // 16]

        x_bytes = keep.tile([P, T], U8, name="x_bytes")
        d_bytes = keep.tile([P, G], U8, name="d_bytes")

        def load_scales(tile, scales):
            rows = scales[0].bitcast(I32)
            nc.scalar.dma_start(tile[:].bitcast(I32), rows.unsqueeze(1).to_broadcast([16, 8, rows.shape[1]]))

        load_scales(x_bytes, x_scales)
        l_offs, l_two = load_list(offs, "l_offs"), load_list(two, "l_two")
        load_scales(d_bytes, d_scales)
        l_k1, l_k2 = load_list(k1, "l_k1"), load_list(k2, "l_k2")

        x_table = keep.tile([P, T], U32, name="x_table")
        d_table = keep.tile([P, G], U32, name="d_table")
        nc.sync.dma_start(d_table[:].bitcast(I32), d_words[0].rearrange("p n t -> p (n t)").bitcast(I32))
        nc.sync.dma_start(x_table[:].bitcast(I32), x_words[0].rearrange("p n t -> p (n t)").bitcast(I32))

        l_n1, l_n2 = load_list(n1, "l_n1"), load_list(n2, "l_n2")
        gs_raw = keep.tile([P, PACK], F32, name="gs_raw")
        nc.sync.dma_start(gs_raw[:], gs.rearrange("(p t) o -> p (t o)", t=PACK))
        gain = keep.tile([P, PACK], F32, name="gain")
        nc.vector.tensor_scalar(gain[:], gs_raw[:], SIXTEENTH, None, ALU.mult)
        l_n3, l_n4 = load_list(n3, "l_n3"), load_list(n4, "l_n4")
        l_k3, l_k4, l_hz = load_list(k3, "l_k3"), load_list(k4, "l_k4"), load_list(hz, "l_hz")
        l_n5 = load_list(n5, "l_n5")
        l_n6, l_n7 = load_list(n6, "l_n6"), load_list(n7, "l_n7")
        l_n8, l_n9, l_n10 = load_list(n8, "l_n8"), load_list(n9, "l_n9"), load_list(n10, "l_n10")

        def gather(dst, picks):
            col = 0
            for table, offsets in picks:
                count = 16 * offsets.shape[1]
                nc.vector.tensor_copy(dst[:, col : col + count], table[:].indirect(offsets))
                col = col + count

        def place_rows(dst, src, queues):
            for j in range(4):
                queues[j % len(queues)].dma_start(dst[j:P:32, :].bitcast(I32), src[8 * j : P : 32, :].bitcast(I32))

        wide1 = 2 * S + 2 * H
        bytes1 = shared.tile([P, wide1], U8, name="bytes1", align_bytes=64, offset=0)
        plane1 = keep.tile([P, wide1], U8, name="plane1", align_bytes=64)
        nc.vector.memset(plane1[:].bitcast(I32), 0)
        gather(bytes1, [(x_bytes, l_offs[:]), (x_bytes, l_two[:]), (d_bytes, l_k1[:]), (d_bytes, l_k2[:])])
        place_rows(plane1, bytes1, [nc.scalar])
        dw1 = keep.tile([P, 2 * H], U32, name="dw1")
        gather(dw1, [(d_table, l_k1[:]), (d_table, l_k2[:])])
        dealt_words = [
            keep.tile([P, 2, 2, P], U32, name="dealt_words0", align_bytes=64),
            shared.tile([P, 2, 2, P], U32, name="dealt_words1", align_bytes=64, offset=4 * S),
        ]
        dealt_bytes = [keep.tile([P, 2, 2, P], U8, name="dealt_bytes%d" % i, align_bytes=64) for i in range(2)]

        def deal(i):
            tiles = slice(2 * i, 2 * i + 2)
            nc.vector.tensor_copy(
                dealt_words[i][:].bitcast(I32).rearrange("p a t m -> p a m t"),
                dw1[:].bitcast(I32).rearrange("p (a m t) -> p a m t", a=2, t=PACK)[:, :, :, tiles],
            )
            nc.vector.tensor_copy(
                dealt_bytes[i][:].rearrange("p a t m -> p a m t"),
                plane1[:, 2 * S :].rearrange("p (a m t) -> p a m t", a=2, t=PACK)[:, :, :, tiles],
            )

        xw_offs = keep.tile([P, S], U32, name="xw_offs", align_bytes=64)
        xw_two = shared.tile([P, S], U32, name="xw_two", align_bytes=64, offset=0)
        xw1 = [xw_offs, xw_two]
        deal(0)
        gather(xw_offs, [(x_table, l_offs[:])])
        gather(xw_two, [(x_table, l_two[:])])
        deal(1)
        banks = [psum.tile([P, S], F32, name="h_bank%d" % t, tag="bank%d" % t) for t in range(TILES)]
        passes = [(0, a, t) for a in range(2) for t in range(2)] + [(1, a, t) for t in range(2) for a in range(2)]
        for i, a, t in passes:
            nc.tensor.matmul_mx(
                out=banks[2 * i + t][:],
                lhsT=dealt_words[i][:, a, t, :].bitcast(FP8X4),
                lhsT_scale=dealt_bytes[i][:, a, t, :],
                rhs=xw1[a][:].bitcast(FP8X4),
                rhs_scale=plane1[:, a * S : (a + 1) * S],
                start=(a == 0),
                stop=(a == 1),
            )

        pab = [
            later.tile([P, 2, 2, W], F32, name="pab0", align_bytes=64, offset=256),
            keep.tile([P, 2, 2, W], F32, name="pab1"),
        ]
        ra = keep.tile([P, TILES, W], F32, name="ra")
        rb = keep.tile([P, TILES, W], F32, name="rb")
        for t in range(TILES):
            h_t = keep.tile([P, S], F32, name="h%d" % t)
            if t == 0:
                nc.scalar.activation(h_t[:], banks[t][:], COPY)
            else:
                nc.vector.tensor_copy(h_t[:], banks[t][:])
            nc.scalar.activation(pab[t // 2][:, 0, t % 2, :], h_t[:].indirect(l_n1[:]), COPY)
            nc.scalar.activation(pab[t // 2][:, 1, t % 2, :], h_t[:].indirect(l_n2[:]), COPY)

        def combine(i):
            two_tiles = slice(2 * i, 2 * i + 2)
            nc.vector.tensor_tensor(ra[:, two_tiles, :], pab[i][:, 0], pab[i][:, 1], ALU.subtract)
            nc.vector.tensor_tensor(rb[:, two_tiles, :], pab[i][:, 0], pab[i][:, 1], ALU.min)

        combine(0)
        ubs = [keep.tile([P, WINDOW], F32, name="ub%d" % t) for t in range(TILES)]
        last = TILES - 1
        far = keep.tile([P, 2, 2, W], F32, name="far")
        top = keep.tile([P, 2, TILES, W], F32, name="top")

        def put_ra(t):
            nc.scalar.activation(ubs[t][:].indirect(l_n3[:]), ra[:, t, :], COPY)

        def put_rb(t):
            nc.scalar.activation(ubs[t][:].indirect(l_n4[:]), rb[:, t, :], COPY)


        wide2 = S + 2 * H
        bytes2 = later.tile([P, wide2], U8, name="bytes2", align_bytes=64, offset=0)
        plane2 = keep.tile([P, wide2], U8, name="plane2", align_bytes=64)
        nc.vector.memset(plane2[:].bitcast(I32), 0)
        gather(bytes2, [(x_bytes, l_hz[:]), (d_bytes, l_k4[:]), (d_bytes, l_k3[:])])
        place_rows(plane2, bytes2, [nc.sync])
        combine(1)
        part = H // 2
        words2 = later.tile([P, S + 2 * part], U32, name="words2", align_bytes=64, offset=wide2)
        gather(words2, [(x_table, l_hz[:]), (d_table, entries(l_k4, 0, part)), (d_table, entries(l_k3, 0, part))])

        halves = [slice(0, W), slice(W, S)]
        groups2 = [(0, halves[0]), (0, halves[1])] + [(t, slice(0, S)) for t in range(1, TILES)]
        banks2 = [
            psum.tile([P, cols.stop - cols.start], F32, name="h2_bank%d" % g, tag="bank%d" % ((TILES + g) % 8))
            for g, (t, cols) in enumerate(groups2)
        ]

        def hashed_pass(g, words):
            t, cols = groups2[g]
            nc.tensor.matmul_mx(
                out=banks2[g][:],
                lhsT=words.bitcast(FP8X4),
                lhsT_scale=plane2[:, S + t * P : S + (t + 1) * P],
                rhs=words2[:, cols].bitcast(FP8X4),
                rhs_scale=plane2[:, cols],
                start=True,
                stop=False,
            )

        def z_pass(g, words):
            t, cols = groups2[g]
            nc.tensor.matmul_mx(
                out=banks2[g][:],
                lhsT=words.bitcast(FP8X4),
                lhsT_scale=plane2[:, S + H + t * P : S + H + (t + 1) * P],
                rhs=z_words[:, cols].bitcast(FP8X4),
                rhs_scale=z_plane[:, cols],
                start=False,
                stop=True,
            )
            if t == 0:
                nc.scalar.activation(h2s[t][:, cols], banks2[g][:], COPY, scale=SIXTEENTH)
            else:
                nc.vector.tensor_scalar(h2s[t][:, cols], banks2[g][:], SIXTEENTH, None, ALU.mult)

        early = [g for g, (t, cols) in enumerate(groups2) if t < 2]
        late = [g for g, (t, cols) in enumerate(groups2) if t >= 2]
        for g in early:
            t = groups2[g][0]
            hashed_pass(g, words2[:, S + t * P : S + (t + 1) * P])
        z_words = keep.tile([P, S], U32, name="z_words", align_bytes=64)
        z_plane = keep.tile([P, S], U8, name="z_plane", align_bytes=64)
        h2s = [keep.tile([P, WINDOW], F32, name="h2_%d" % t) for t in range(TILES)]

        z_bf = [keep.tile([P, W, PACK], BF16, name="z_bf%d" % half, tag="z_bf%d" % half, align_bytes=64) for half in range(2)]

        def larger_half(t, half):
            nc.scalar.activation(far[:, half, t - 2, :], ubs[t][:].indirect(entries(l_n5, half * W, W)), COPY)
            nc.vector.tensor_tensor(top[:, half, t, :], ubs[t][:, half * W : (half + 1) * W], far[:, half, t - 2, :], ALU.max)

        def weigh(i, half):
            tiles = slice(2 * i, 2 * i + 2)
            nc.vector.tensor_tensor(
                z_bf[half][:, :, tiles],
                top[:, half, tiles, :].rearrange("p t c -> p c t"),
                gain[:, tiles].unsqueeze(1).to_broadcast([P, W, 2]),
                ALU.mult,
            )

        def larger_whole(t):
            far_t = keep.tile([P, S], F32, name="far_t%d" % t)
            nc.scalar.activation(far_t[:], ubs[t][:].indirect(l_n5[:]), COPY)
            nc.vector.tensor_tensor(
                top[:, :, t, :],
                ubs[t][:, 0:S].rearrange("p (a c) -> p a c", a=2),
                far_t[:].rearrange("p (a c) -> p a c", a=2),
                ALU.max,
            )

        put_ra(0)
        put_ra(1)
        put_rb(0)
        put_rb(1)
        larger_whole(0)
        put_ra(2)
        larger_whole(1)
        for half in range(2):
            weigh(0, half)
        put_ra(3)
        put_rb(2)
        put_rb(3)
        for half in range(2):
            larger_half(2, half)
            larger_half(3, half)
            weigh(1, half)
            nc.vector.quantize_mx(
                out=z_words[:, halves[half]].bitcast(FP8X4),
                scales=z_plane[:, halves[half]],
                in_=z_bf[half][:].rearrange("p c t -> p (c t)"),
            )
        for g in early:
            t = groups2[g][0]
            z_pass(g, words2[:, S + part + t * P : S + part + (t + 1) * P])
        words_late = keep.tile([P, 2 * part], U32, name="words_late", tag="z_bf1", align_bytes=64)
        gather(words_late, [(d_table, entries(l_k4, part, part)), (d_table, entries(l_k3, part, part))])
        for g in late:
            t = groups2[g][0] - 2
            hashed_pass(g, words_late[:, t * P : (t + 1) * P])
            z_pass(g, words_late[:, part + t * P : part + (t + 1) * P])

        pa2 = keep.tile([P, TILES, W], F32, name="pa2")
        pb2 = keep.tile([P, TILES, W], F32, name="pb2")
        rb2 = keep.tile([P, TILES, W], F32, name="rb2")
        ub2s = [keep.tile([P, S], F32, name="ub2_%d" % t) for t in range(TILES)]

        def pair_up(t):
            nc.scalar.activation(pa2[:, t, :], h2s[t][:].indirect(l_n6[:]), COPY)
            nc.scalar.activation(pb2[:, t, :], h2s[t][:].indirect(l_n7[:]), COPY)
            nc.vector.tensor_tensor(rb2[:, t, :], pa2[:, t, :], pb2[:, t, :], ALU.max)

        def finish(t):
            ub2 = ub2s[t]
            far2 = keep.tile([P, S], F32, name="far2_%d" % t)
            res = keep.tile([P, S], F32, name="res%d" % t)
            pieces = [slice(0, S)] if t < last else [slice(0, W), slice(W, S)]
            nc.scalar.activation(ub2[:].indirect(l_n8[:]), pb2[:, t, :], COPY)
            first = pieces[0]
            nc.scalar.activation(far2[:, first], h2s[t][:].indirect(entries(l_n10, first.start, first.stop - first.start)), COPY)
            nc.scalar.activation(ub2[:].indirect(l_n9[:]), rb2[:, t, :], COPY)
            for cols in pieces[1:]:
                nc.scalar.activation(far2[:, cols], h2s[t][:].indirect(entries(l_n10, cols.start, cols.stop - cols.start)), COPY)
            for cols in pieces:
                nc.vector.tensor_tensor(res[:, cols], ub2[:, cols], far2[:, cols], ALU.subtract)
                nc.sync.dma_start(out[t * P : (t + 1) * P, cols], res[:, cols])

        pair_up(0)
        for t in range(TILES):
            if t < last:
                pair_up(t + 1)
            finish(t)
